import numpy as np
import ml_dtypes


def mxq(x, axis, fmt="e4m3"):
    dtype, down = {"e4m3": (ml_dtypes.float8_e4m3fn, 7), "e5m2": (ml_dtypes.float8_e5m2, 14)}[fmt]
    v = np.moveaxis(np.asarray(x, np.float32).astype(ml_dtypes.bfloat16).astype(np.float64), axis, -1)
    blocks = v.reshape(v.shape[:-1] + (-1, 32))
    amax = np.abs(blocks).max(-1, keepdims=True)
    byte = np.maximum(np.where(amax > 0, np.frexp(amax)[1] - 1 + 127, 0) - down, 1)
    scale = np.exp2(byte - 127.0)
    codes = (blocks / scale).astype(np.float32).astype(dtype).astype(np.float64)
    return np.moveaxis((codes * scale).reshape(v.shape), -1, axis)


WIDE = False


def mx_kscale(k, group=512):
    if not WIDE:
        return np.ones(k)
    levels = np.array([18, -18])
    if group != 512:
        return np.exp2(np.random.permutation(np.resize(levels, k // group))).repeat(group)
    if k % 512:
        return np.exp2(np.random.permutation(np.resize(levels, k // 32))).repeat(32)
    a = np.empty((k // 512, 16))
    for p in range(k // 512):
        a[p, :8] = np.random.permutation(np.resize(levels, 8))
        for g in range(8):
            far = levels[np.abs(levels - a[p, g]) >= 10]
            a[p, g + 8] = far[np.random.randint(len(far))]
    return np.exp2(a.ravel()).repeat(32)


def f64(x):
    return np.asarray(x).astype(np.float64)


H, D, N = 4, 128, 512


def setup_inputs():
    n = np.random.standard_normal
    s = mx_kscale(D, 0)[:, None]
    S = n((H, D, 128)) / np.sqrt(D)
    return {
        "q": n((H, D, N)).astype(np.float32),
        "qa": (np.random.uniform(0.5, 2.0, (D, 1)) * s).astype(np.float32),
        "S": (S / s).astype(np.float32),
    }


def reference(q, qa, S):
    fq = (np.where(f64(q) > 0, f64(q) + 1.0, np.exp(np.minimum(f64(q), 0.0)))) * f64(qa)
    y = mxq(fq, 1, "e4m3").transpose(0, 2, 1) @ mxq(f64(S), 1, "e4m3")
    return y

@@ -1,0 +1,180 @@
+from contextlib import ExitStack
+
+import concourse.mybir as mybir
+
+H, D, N, E = 4, 128, 512, 128
+FLOPS = 2 * H * D * N * E
+
+F32 = mybir.dt.float32
+BF16 = mybir.dt.bfloat16
+U32 = mybir.dt.uint32
+U8 = mybir.dt.uint8
+FP8X4 = mybir.dt.float8_e4m3fn_x4
+ALU = mybir.AluOpType
+ACT = mybir.ActivationFunctionType
+
+P = 128
+PACK = 4
+ROWS = D // PACK
+T = 128
+CHUNKS = N // T
+RUN = 2
+
+
+def tile_rows_read_elu1_kernel(tc, q, qa, S, out):
+    nc = tc.nc
+    q_src = q.rearrange("h (p j) n -> (h p) j n", j=PACK)
+    s_src = S.rearrange("h (p j) e -> (h p) j e", j=PACK)
+    out_dst = out.rearrange("h n e -> n h e")
+
+    with ExitStack() as ctx:
+        sb = ctx.enter_context(tc.tile_pool(name="sb", bufs=1))
+        ps = ctx.enter_context(tc.psum_pool(name="ps", bufs=1))
+
+        def tiles(name, shape, dtype):
+            return [sb.tile(shape, dtype, name=name + str(c), align_bytes=64) for c in range(CHUNKS)]
+
+        raw = tiles("raw", [P, PACK, T], F32)
+        neg = tiles("neg", [P, PACK, T], F32)
+        expo = tiles("expo", [P, PACK, T], F32)
+        phi = tiles("phi", [P, PACK, T], F32)
+        grouped = tiles("grouped", [P, T, PACK], BF16)
+        codes = tiles("codes", [P, T], U32)
+        scales = tiles("scales", [P, T], U8)
+        res = tiles("res", [P, H, E], F32)
+        weight = sb.tile([P, PACK], F32, name="weight", align_bytes=64)
+        s_raw = sb.tile([P, PACK, E], F32, name="s_raw", align_bytes=64)
+        s_grouped = sb.tile([P, E, PACK], BF16, name="s_grouped", align_bytes=64)
+        s_codes = sb.tile([P, E], U32, name="s_codes", align_bytes=64)
+        s_scales = sb.tile([P, E], U8, name="s_scales", align_bytes=64)
+        banks = [[ps.tile([P, 512], F32, name="bank%d_%d" % (h, b)) for b in range(2)] for h in range(H)]
+
+        def load(c, js=slice(0, PACK)):
+            nc.sync.dma_start(out=raw[c][:, js, :], in_=q_src[:, js, c * T : (c + 1) * T])
+
+        def clamp_v(c, js=slice(0, PACK)):
+            nc.vector.tensor_scalar(out=neg[c][:, js, :], in0=raw[c][:, js, :], scalar1=0.0, scalar2=None, op0=ALU.min)
+
+        def exp_of_min(c, js=slice(0, PACK)):
+            nc.scalar.activation(out=expo[c][:, js, :], in_=neg[c][:, js, :], func=ACT.Exp)
+
+        def clamp_s(c):
+            nc.scalar.activation(out=neg[c][:], in_=raw[c][:], func=ACT.Relu, scale=-1.0)
+
+        def exp_of_relu(c):
+            nc.scalar.activation(out=expo[c][:], in_=neg[c][:], func=ACT.Exp, scale=-1.0)
+
+        def combine(c, js=slice(0, PACK)):
+            nc.vector.scalar_tensor_tensor(
+                out=phi[c][:, js, :], in0=raw[c][:, js, :], scalar=1.0, in1=expo[c][:, js, :], op0=ALU.add, op1=ALU.max
+            )
+
+        def weigh(c):
+            nc.vector.tensor_tensor(
+                out=grouped[c][:].rearrange("p (g i) j -> p g j i", i=RUN),
+                in0=phi[c][:].rearrange("p j (g i) -> p g j i", i=RUN),
+                in1=weight[:].unsqueeze(1).unsqueeze(3).broadcast_to([P, T // RUN, PACK, RUN]),
+                op=ALU.mult,
+            )
+
+        def quantize(c):
+            nc.vector.quantize_mx(
+                out=codes[c][:].bitcast(FP8X4), scales=scales[c][:], in_=grouped[c][:].rearrange("p n j -> p (n j)")
+            )
+
+        def acc(c, h):
+            return banks[h][c % 2][:, (c // 2) * E : (c // 2 + 1) * E]
+
+        def multiply(c):
+            for h in range(H):
+                rows = slice(ROWS * h, ROWS * (h + 1))
+                nc.tensor.matmul_mx(
+                    out=acc(c, h),
+                    lhsT=codes[c][rows, :].bitcast(FP8X4),
+                    lhsT_scale=scales[c][rows, :],
+                    rhs=s_codes[rows, :].bitcast(FP8X4),
+                    rhs_scale=s_scales[rows, :],
+                    start=True,
+                    stop=True,
+                )
+
+        def empty_s(c, heads):
+            for h in heads:
+                nc.scalar.copy(out=res[c][:, h, :], in_=acc(c, h))
+
+        def empty_v(c, heads):
+            for h in heads:
+                nc.vector.tensor_copy(out=res[c][:, h, :], in_=acc(c, h))
+
+        def store(c, hs=slice(0, H)):
+            nc.sync.dma_start(out=out_dst[c * T : (c + 1) * T, hs, :], in_=res[c][:, hs, :])
+
+        def s_interleave():
+            nc.scalar.copy(
+                out=s_grouped[:].rearrange("p (g i) j -> p g j i", i=RUN),
+                in_=s_raw[:].rearrange("p j (g i) -> p g j i", i=RUN),
+            )
+
+        def s_quantize():
+            nc.vector.quantize_mx(
+                out=s_codes[:].bitcast(FP8X4), scales=s_scales[:], in_=s_grouped[:].rearrange("p e j -> p (e j)")
+            )
+
+        lo, hi = slice(0, 2), slice(2, 4)
+        with tc.manual_schedule():
+            load(0, lo)
+            load(0, hi)
+            load(1, lo)
+            load(1, hi)
+            nc.sync.dma_start(out=weight[:], in_=qa.rearrange("(p j) o -> p (j o)", j=PACK).partition_broadcast(H))
+            load(2)
+            nc.sync.dma_start(out=s_raw[:], in_=s_src)
+            load(3)
+
+            clamp_v(0, lo)
+            exp_of_min(0, lo)
+            clamp_v(0, hi)
+            exp_of_min(0, hi)
+            clamp_v(1, lo)
+            exp_of_min(1, lo)
+            combine(0, lo)
+            clamp_v(1, hi)
+            exp_of_min(1, hi)
+            combine(0, hi)
+            combine(1, lo)
+            weigh(0)
+            combine(1, hi)
+            quantize(0)
+            clamp_s(2)
+            s_interleave()
+            exp_of_relu(2)
+            s_quantize()
+            multiply(0)
+            weigh(1)
+            clamp_s(3)
+            empty_s(0, [0])
+            exp_of_relu(3)
+            combine(2)
+            quantize(1)
+            multiply(1)
+            empty_s(0, [1, 2, 3])
+            store(0)
+            weigh(2)
+            combine(3)
+            quantize(2)
+            empty_s(1, range(H))
+            store(1)
+            multiply(2)
+            weigh(3)
+            empty_s(2, [0])
+            empty_v(2, [1])
+            empty_s(2, [2, 3])
+            store(2)
+            quantize(3)
+            multiply(3)
+            empty_v(3, [0])
+            empty_s(3, [1])
+            store(3, lo)
+            empty_v(3, [2])
+            empty_s(3, [3])
+            store(3, hi)

@@ -17,7 +17,6 @@ P = 128
 PACK = 4
 ROWS = D // PACK
 T = 128
-CHUNKS = N // T
 RUN = 2
 
 
@@ -25,89 +24,104 @@ def tile_rows_read_elu1_kernel(tc, q, qa, S, out):
     nc = tc.nc
     q_src = q.rearrange("h (p j) n -> (h p) j n", j=PACK)
     s_src = S.rearrange("h (p j) e -> (h p) j e", j=PACK)
-    out_dst = out.rearrange("h n e -> n h e")
+    w_src = qa.rearrange("(p j) o -> p (j o)", j=PACK)
+    spans = [(0, 2 * T), (2 * T, T), (3 * T, T)]
 
     with ExitStack() as ctx:
         sb = ctx.enter_context(tc.tile_pool(name="sb", bufs=1))
         ps = ctx.enter_context(tc.psum_pool(name="ps", bufs=1))
 
         def tiles(name, shape, dtype):
-            return [sb.tile(shape, dtype, name=name + str(c), align_bytes=64) for c in range(CHUNKS)]
+            return [sb.tile(shape(w), dtype, name=name + str(g), align_bytes=64) for g, (n0, w) in enumerate(spans)]
 
-        raw = tiles("raw", [P, PACK, T], F32)
-        neg = tiles("neg", [P, PACK, T], F32)
-        expo = tiles("expo", [P, PACK, T], F32)
-        phi = tiles("phi", [P, PACK, T], F32)
-        grouped = tiles("grouped", [P, T, PACK], BF16)
-        codes = tiles("codes", [P, T], U32)
-        scales = tiles("scales", [P, T], U8)
-        res = tiles("res", [P, H, E], F32)
+        raw = tiles("raw", lambda w: [P, PACK, w], F32)
+        neg = tiles("neg", lambda w: [P, PACK, w], F32)
+        expo = tiles("expo", lambda w: [P, PACK, w], F32)
+        phi = tiles("phi", lambda w: [P, PACK, w], F32)
+        grouped = tiles("grouped", lambda w: [P, w, PACK], BF16)
+        codes = tiles("codes", lambda w: [P, w], U32)
+        scales = tiles("scales", lambda w: [P, w], U8)
+        res = tiles("res", lambda w: [P, H, (w // T) * E], F32)
         weight = sb.tile([P, PACK], F32, name="weight", align_bytes=64)
         s_raw = sb.tile([P, PACK, E], F32, name="s_raw", align_bytes=64)
         s_grouped = sb.tile([P, E, PACK], BF16, name="s_grouped", align_bytes=64)
         s_codes = sb.tile([P, E], U32, name="s_codes", align_bytes=64)
         s_scales = sb.tile([P, E], U8, name="s_scales", align_bytes=64)
         banks = [[ps.tile([P, 512], F32, name="bank%d_%d" % (h, b)) for b in range(2)] for h in range(H)]
+        acc = [
+            [banks[h][0][:, 0 : 2 * E] for h in range(H)],
+            [banks[h][1][:, 0:E] for h in range(H)],
+            [banks[h][0][:, 2 * E : 3 * E] for h in range(H)],
+        ]
 
-        def load(c, js=slice(0, PACK)):
-            nc.sync.dma_start(out=raw[c][:, js, :], in_=q_src[:, js, c * T : (c + 1) * T])
+        def load(g, js=slice(0, PACK)):
+            n0, w = spans[g]
+            nc.sync.dma_start(out=raw[g][:, js, :], in_=q_src[:, js, n0 : n0 + w])
 
-        def clamp_v(c, js=slice(0, PACK)):
-            nc.vector.tensor_scalar(out=neg[c][:, js, :], in0=raw[c][:, js, :], scalar1=0.0, scalar2=None, op0=ALU.min)
+        def load_weight(engine, h):
+            engine.dma_start(out=weight[ROWS * h : ROWS * (h + 1), :], in_=w_src)
 
-        def exp_of_min(c, js=slice(0, PACK)):
-            nc.scalar.activation(out=expo[c][:, js, :], in_=neg[c][:, js, :], func=ACT.Exp)
+        def clamp_v(g, js):
+            nc.vector.tensor_scalar(out=neg[g][:, js, :], in0=raw[g][:, js, :], scalar1=0.0, scalar2=None, op0=ALU.min)
 
-        def clamp_s(c):
-            nc.scalar.activation(out=neg[c][:], in_=raw[c][:], func=ACT.Relu, scale=-1.0)
+        def exp_of_min(g, js):
+            nc.scalar.activation(out=expo[g][:, js, :], in_=neg[g][:, js, :], func=ACT.Exp)
 
-        def exp_of_relu(c):
-            nc.scalar.activation(out=expo[c][:], in_=neg[c][:], func=ACT.Exp, scale=-1.0)
+        def clamp_s(g, js):
+            nc.scalar.activation(out=neg[g][:, js, :], in_=raw[g][:, js, :], func=ACT.Relu, scale=-1.0)
 
-        def combine(c, js=slice(0, PACK)):
+        def exp_of_relu(g, js):
+            nc.scalar.activation(out=expo[g][:, js, :], in_=neg[g][:, js, :], func=ACT.Exp, scale=-1.0)
+
+        def combine(g, js):
             nc.vector.scalar_tensor_tensor(
-                out=phi[c][:, js, :], in0=raw[c][:, js, :], scalar=1.0, in1=expo[c][:, js, :], op0=ALU.add, op1=ALU.max
+                out=phi[g][:, js, :], in0=raw[g][:, js, :], scalar=1.0, in1=expo[g][:, js, :], op0=ALU.add, op1=ALU.max
             )
 
-        def weigh(c):
+        def weigh(g):
+            if g == 0:
+                dst = grouped[g][:].rearrange("p (r s) j -> p s j r", r=RUN)
+            else:
+                dst = grouped[g][:].rearrange("p (s r) j -> p s j r", r=RUN)
             nc.vector.tensor_tensor(
-                out=grouped[c][:].rearrange("p (g i) j -> p g j i", i=RUN),
-                in0=phi[c][:].rearrange("p j (g i) -> p g j i", i=RUN),
-                in1=weight[:].unsqueeze(1).unsqueeze(3).broadcast_to([P, T // RUN, PACK, RUN]),
+                out=dst,
+                in0=phi[g][:].rearrange("p j (s r) -> p s j r", r=RUN),
+                in1=weight[:].unsqueeze(1).unsqueeze(3).broadcast_to([P, spans[g][1] // RUN, PACK, RUN]),
                 op=ALU.mult,
             )
 
-        def quantize(c):
+        def quantize(g):
             nc.vector.quantize_mx(
-                out=codes[c][:].bitcast(FP8X4), scales=scales[c][:], in_=grouped[c][:].rearrange("p n j -> p (n j)")
+                out=codes[g][:].bitcast(FP8X4), scales=scales[g][:], in_=grouped[g][:].rearrange("p n j -> p (n j)")
             )
 
-        def acc(c, h):
-            return banks[h][c % 2][:, (c // 2) * E : (c // 2 + 1) * E]
-
-        def multiply(c):
+        def multiply(g):
             for h in range(H):
                 rows = slice(ROWS * h, ROWS * (h + 1))
-                nc.tensor.matmul_mx(
-                    out=acc(c, h),
-                    lhsT=codes[c][rows, :].bitcast(FP8X4),
-                    lhsT_scale=scales[c][rows, :],
-                    rhs=s_codes[rows, :].bitcast(FP8X4),
-                    rhs_scale=s_scales[rows, :],
-                    start=True,
-                    stop=True,
-                )
+                for r in range(spans[g][1] // T):
+                    cols = slice(r * T, (r + 1) * T)
+                    nc.tensor.matmul_mx(
+                        out=acc[g][h][:, r * E : (r + 1) * E],
+                        lhsT=codes[g][rows, cols].bitcast(FP8X4),
+                        lhsT_scale=scales[g][rows, cols],
+                        rhs=s_codes[rows, :].bitcast(FP8X4),
+                        rhs_scale=s_scales[rows, :],
+                        start=True,
+                        stop=True,
+                    )
 
-        def empty_s(c, heads):
+        def empty_s(g, heads):
             for h in heads:
-                nc.scalar.copy(out=res[c][:, h, :], in_=acc(c, h))
+                nc.scalar.copy(out=res[g][:, h, :], in_=acc[g][h])
 
-        def empty_v(c, heads):
+        def empty_v(g, heads):
             for h in heads:
-                nc.vector.tensor_copy(out=res[c][:, h, :], in_=acc(c, h))
+                nc.vector.tensor_copy(out=res[g][:, h, :], in_=acc[g][h])
 
-        def store(c, hs=slice(0, H)):
-            nc.sync.dma_start(out=out_dst[c * T : (c + 1) * T, hs, :], in_=res[c][:, hs, :])
+        def store(g, hs=slice(0, H), engine=nc.sync):
+            n0, w = spans[g]
+            dst = out[:, n0 : n0 + w, :].rearrange("h (s r) e -> s h (r e)", r=w // T)
+            engine.dma_start(out=dst[:, hs, :], in_=res[g][:, hs, :])
 
         def s_interleave():
             nc.scalar.copy(
@@ -121,60 +135,56 @@ def tile_rows_read_elu1_kernel(tc, q, qa, S, out):
             )
 
         lo, hi = slice(0, 2), slice(2, 4)
+        planes = [slice(j, j + 1) for j in range(PACK)]
         with tc.manual_schedule():
-            load(0, lo)
-            load(0, hi)
-            load(1, lo)
-            load(1, hi)
-            nc.sync.dma_start(out=weight[:], in_=qa.rearrange("(p j) o -> p (j o)", j=PACK).partition_broadcast(H))
-            load(2)
+            load_weight(nc.scalar, 0)
+            load_weight(nc.scalar, 1)
+            load_weight(nc.gpsimd, 2)
+            load_weight(nc.gpsimd, 3)
+            for js in planes:
+                load(0, js)
             nc.sync.dma_start(out=s_raw[:], in_=s_src)
-            load(3)
-
-            clamp_v(0, lo)
-            exp_of_min(0, lo)
-            clamp_v(0, hi)
-            exp_of_min(0, hi)
-            clamp_v(1, lo)
-            exp_of_min(1, lo)
-            combine(0, lo)
-            clamp_v(1, hi)
-            exp_of_min(1, hi)
-            combine(0, hi)
-            combine(1, lo)
-            weigh(0)
-            combine(1, hi)
-            quantize(0)
-            clamp_s(2)
+            load(1)
+            load(2)
+            for js in planes:
+                clamp_v(0, js)
+                exp_of_min(0, js)
+            for js in planes:
+                combine(0, js)
             s_interleave()
-            exp_of_relu(2)
             s_quantize()
+            weigh(0)
+            clamp_s(1, lo)
+            clamp_s(1, hi)
+            exp_of_relu(1, lo)
+            clamp_s(2, lo)
+            exp_of_relu(1, hi)
+            clamp_s(2, hi)
+            exp_of_relu(2, lo)
+            exp_of_relu(2, hi)
+            combine(1, lo)
+            quantize(0)
             multiply(0)
+            combine(1, hi)
+            combine(2, lo)
             weigh(1)
-            clamp_s(3)
-            empty_s(0, [0])
-            exp_of_relu(3)
-            combine(2)
+            combine(2, hi)
             quantize(1)
             multiply(1)
-            empty_s(0, [1, 2, 3])
-            store(0)
+            empty_s(0, [0, 1])
+            store(0, lo)
+            empty_s(0, [2, 3])
+            store(0, hi)
             weigh(2)
-            combine(3)
-            quantize(2)
-            empty_s(1, range(H))
+            empty_s(1, [0])
+            empty_v(1, [1])
+            empty_s(1, [2, 3])
             store(1)
+            quantize(2)
             multiply(2)
-            weigh(3)
             empty_s(2, [0])
             empty_v(2, [1])
-            empty_s(2, [2, 3])
-            store(2)
-            quantize(3)
-            multiply(3)
-            empty_v(3, [0])
-            empty_s(3, [1])
-            store(3, lo)
-            empty_v(3, [2])
-            empty_s(3, [3])
-            store(3, hi)
+            store(2, lo)
+            empty_s(2, [2])
+            empty_v(2, [3])
+            store(2, hi)

@@ -58,8 +58,8 @@ def tile_rows_read_elu1_kernel(tc, q, qa, S, out):
             n0, w = spans[g]
             nc.sync.dma_start(out=raw[g][:, js, :], in_=q_src[:, js, n0 : n0 + w])
 
-        def load_weight(engine, h):
-            engine.dma_start(out=weight[ROWS * h : ROWS * (h + 1), :], in_=w_src)
+        def load_weight():
+            nc.sync.dma_start(out=weight[:], in_=w_src.partition_broadcast(H))
 
         def clamp_v(g, js):
             nc.vector.tensor_scalar(out=neg[g][:, js, :], in0=raw[g][:, js, :], scalar1=0.0, scalar2=None, op0=ALU.min)
@@ -137,13 +137,10 @@ def tile_rows_read_elu1_kernel(tc, q, qa, S, out):
         lo, hi = slice(0, 2), slice(2, 4)
         planes = [slice(j, j + 1) for j in range(PACK)]
         with tc.manual_schedule():
-            load_weight(nc.scalar, 0)
-            load_weight(nc.scalar, 1)
-            load_weight(nc.gpsimd, 2)
-            load_weight(nc.gpsimd, 3)
             for js in planes:
                 load(0, js)
             nc.sync.dma_start(out=s_raw[:], in_=s_src)
+            load_weight()
             load(1)
             load(2)
             for js in planes:

@@ -18,6 +18,7 @@ PACK = 4
 ROWS = D // PACK
 T = 128
 RUN = 2
+HALF = N // 2
 
 
 def tile_rows_read_elu1_kernel(tc, q, qa, S, out):
@@ -31,13 +32,16 @@ def tile_rows_read_elu1_kernel(tc, q, qa, S, out):
         sb = ctx.enter_context(tc.tile_pool(name="sb", bufs=1))
         ps = ctx.enter_context(tc.psum_pool(name="ps", bufs=1))
 
+        def halves(name):
+            return [sb.tile([P, PACK, HALF], F32, name=name + str(u), align_bytes=64) for u in range(2)]
+
         def tiles(name, shape, dtype):
             return [sb.tile(shape(w), dtype, name=name + str(g), align_bytes=64) for g, (n0, w) in enumerate(spans)]
 
-        raw = tiles("raw", lambda w: [P, PACK, w], F32)
-        neg = tiles("neg", lambda w: [P, PACK, w], F32)
-        expo = tiles("expo", lambda w: [P, PACK, w], F32)
-        phi = tiles("phi", lambda w: [P, PACK, w], F32)
+        raw = halves("raw")
+        expo = halves("expo")
+        above = halves("above")
+        below = halves("below")
         grouped = tiles("grouped", lambda w: [P, w, PACK], BF16)
         codes = tiles("codes", lambda w: [P, w], U32)
         scales = tiles("scales", lambda w: [P, w], U8)
@@ -54,45 +58,43 @@ def tile_rows_read_elu1_kernel(tc, q, qa, S, out):
             [banks[h][0][:, 2 * E : 3 * E] for h in range(H)],
         ]
 
-        def load(g, js=slice(0, PACK)):
-            n0, w = spans[g]
-            nc.sync.dma_start(out=raw[g][:, js, :], in_=q_src[:, js, n0 : n0 + w])
+        def load(u, js):
+            nc.sync.dma_start(out=raw[u][:, js, :], in_=q_src[:, js, u * HALF : (u + 1) * HALF])
 
-        def load_weight():
-            nc.sync.dma_start(out=weight[:], in_=w_src.partition_broadcast(H))
+        def exp(u, js, ns=slice(0, HALF)):
+            nc.scalar.activation(out=expo[u][:, js, ns], in_=raw[u][:, js, ns], func=ACT.Exp)
 
-        def clamp_v(g, js):
-            nc.vector.tensor_scalar(out=neg[g][:, js, :], in0=raw[g][:, js, :], scalar1=0.0, scalar2=None, op0=ALU.min)
-
-        def exp_of_min(g, js):
-            nc.scalar.activation(out=expo[g][:, js, :], in_=neg[g][:, js, :], func=ACT.Exp)
-
-        def clamp_s(g, js):
-            nc.scalar.activation(out=neg[g][:, js, :], in_=raw[g][:, js, :], func=ACT.Relu, scale=-1.0)
-
-        def exp_of_relu(g, js):
-            nc.scalar.activation(out=expo[g][:, js, :], in_=neg[g][:, js, :], func=ACT.Exp, scale=-1.0)
-
-        def combine(g, js):
-            nc.vector.scalar_tensor_tensor(
-                out=phi[g][:, js, :], in0=raw[g][:, js, :], scalar=1.0, in1=expo[g][:, js, :], op0=ALU.add, op1=ALU.max
+        def weigh_above(u, j):
+            nc.vector.tensor_scalar(
+                out=above[u][:, j, :], in0=raw[u][:, j, :], scalar1=0.0, scalar2=weight[:, j : j + 1],
+                op0=ALU.max, op1=ALU.mult,
             )
 
-        def weigh(g):
+        def weigh_below(u, j, ns=slice(0, HALF)):
+            nc.vector.tensor_scalar(
+                out=below[u][:, j, ns], in0=expo[u][:, j, ns], scalar1=1.0, scalar2=weight[:, j : j + 1],
+                op0=ALU.min, op1=ALU.mult,
+            )
+
+        def join(g, c0, cw):
+            n0, w = spans[g]
+            u, m0 = divmod(n0 + c0, HALF)
             if g == 0:
                 dst = grouped[g][:].rearrange("p (r s) j -> p s j r", r=RUN)
             else:
-                dst = grouped[g][:].rearrange("p (s r) j -> p s j r", r=RUN)
+                dst = grouped[g][:, c0 : c0 + cw, :].rearrange("p (s r) j -> p s j r", r=RUN)
             nc.vector.tensor_tensor(
                 out=dst,
-                in0=phi[g][:].rearrange("p j (s r) -> p s j r", r=RUN),
-                in1=weight[:].unsqueeze(1).unsqueeze(3).broadcast_to([P, spans[g][1] // RUN, PACK, RUN]),
-                op=ALU.mult,
+                in0=above[u][:, :, m0 : m0 + cw].rearrange("p j (s r) -> p s j r", r=RUN),
+                in1=below[u][:, :, m0 : m0 + cw].rearrange("p j (s r) -> p s j r", r=RUN),
+                op=ALU.add,
             )
 
-        def quantize(g):
+        def quantize(g, c0, cw):
             nc.vector.quantize_mx(
-                out=codes[g][:].bitcast(FP8X4), scales=scales[g][:], in_=grouped[g][:].rearrange("p n j -> p (n j)")
+                out=codes[g][:, c0 : c0 + cw].bitcast(FP8X4),
+                scales=scales[g][:, c0 : c0 + cw],
+                in_=grouped[g][:, c0 : c0 + cw, :].rearrange("p n j -> p (n j)"),
             )
 
         def multiply(g):
@@ -137,47 +139,50 @@ def tile_rows_read_elu1_kernel(tc, q, qa, S, out):
         lo, hi = slice(0, 2), slice(2, 4)
         planes = [slice(j, j + 1) for j in range(PACK)]
         with tc.manual_schedule():
+            nc.scalar.dma_start(out=weight[:], in_=w_src.partition_broadcast(H))
             for js in planes:
                 load(0, js)
             nc.sync.dma_start(out=s_raw[:], in_=s_src)
-            load_weight()
-            load(1)
-            load(2)
+            load(1, lo)
+            load(1, hi)
             for js in planes:
-                clamp_v(0, js)
-                exp_of_min(0, js)
-            for js in planes:
-                combine(0, js)
+                exp(0, js)
+            weigh_above(0, 0)
+            for j in range(1, PACK):
+                weigh_above(0, j)
+                weigh_below(0, j - 1)
+            weigh_below(0, PACK - 1)
             s_interleave()
+            exp(1, lo)
+            exp(1, hi, slice(0, T))
+            exp(1, hi, slice(T, HALF))
+            join(0, 0, 2 * T)
             s_quantize()
-            weigh(0)
-            clamp_s(1, lo)
-            clamp_s(1, hi)
-            exp_of_relu(1, lo)
-            clamp_s(2, lo)
-            exp_of_relu(1, hi)
-            clamp_s(2, hi)
-            exp_of_relu(2, lo)
-            exp_of_relu(2, hi)
-            combine(1, lo)
-            quantize(0)
+            weigh_above(1, 0)
+            quantize(0, 0, 2 * T)
             multiply(0)
-            combine(1, hi)
-            combine(2, lo)
-            weigh(1)
-            combine(2, hi)
-            quantize(1)
-            multiply(1)
+            weigh_above(1, 1)
+            weigh_below(1, 0)
+            weigh_below(1, 1)
+            weigh_above(1, 2)
+            weigh_above(1, 3)
+            weigh_below(1, 2, slice(0, T))
+            weigh_below(1, 3, slice(0, T))
+            weigh_below(1, 2, slice(T, HALF))
             empty_s(0, [0, 1])
             store(0, lo)
             empty_s(0, [2, 3])
             store(0, hi)
-            weigh(2)
-            empty_s(1, [0])
-            empty_v(1, [1])
-            empty_s(1, [2, 3])
+            join(1, 0, T)
+            weigh_below(1, 3, slice(T, HALF))
+            quantize(1, 0, T)
+            multiply(1)
+            join(2, 0, T // 2)
+            join(2, T // 2, T // 2)
+            empty_s(1, [0, 1, 2, 3])
             store(1)
-            quantize(2)
+            quantize(2, 0, T // 2)
+            quantize(2, T // 2, T // 2)
             multiply(2)
             empty_s(2, [0])
             empty_v(2, [1])

@@ -80,7 +80,7 @@ def tile_rows_read_elu1_kernel(tc, q, qa, S, out):
             n0, w = spans[g]
             u, m0 = divmod(n0 + c0, HALF)
             if g == 0:
-                dst = grouped[g][:].rearrange("p (r s) j -> p s j r", r=RUN)
+                dst = grouped[g][:].rearrange("p (r s) j -> p s j r", r=RUN)[:, c0 // RUN : (c0 + cw) // RUN]
             else:
                 dst = grouped[g][:, c0 : c0 + cw, :].rearrange("p (s r) j -> p s j r", r=RUN)
             nc.vector.tensor_tensor(
@@ -145,22 +145,26 @@ def tile_rows_read_elu1_kernel(tc, q, qa, S, out):
             nc.sync.dma_start(out=s_raw[:], in_=s_src)
             load(1, lo)
             load(1, hi)
-            for js in planes:
+            for js in planes[:-1]:
                 exp(0, js)
+            exp(0, planes[-1], slice(0, T))
+            exp(0, planes[-1], slice(T, HALF))
             weigh_above(0, 0)
             for j in range(1, PACK):
                 weigh_above(0, j)
                 weigh_below(0, j - 1)
-            weigh_below(0, PACK - 1)
+            weigh_below(0, PACK - 1, slice(0, T))
+            weigh_below(0, PACK - 1, slice(T, HALF))
             s_interleave()
             exp(1, lo)
             exp(1, hi, slice(0, T))
             exp(1, hi, slice(T, HALF))
-            join(0, 0, 2 * T)
+            join(0, 0, T)
+            join(0, T, T)
             s_quantize()
-            weigh_above(1, 0)
             quantize(0, 0, 2 * T)
             multiply(0)
+            weigh_above(1, 0)
             weigh_above(1, 1)
             weigh_below(1, 0)
             weigh_below(1, 1)
@@ -169,18 +173,19 @@ def tile_rows_read_elu1_kernel(tc, q, qa, S, out):
             weigh_below(1, 2, slice(0, T))
             weigh_below(1, 3, slice(0, T))
             weigh_below(1, 2, slice(T, HALF))
-            empty_s(0, [0, 1])
-            store(0, lo)
-            empty_s(0, [2, 3])
-            store(0, hi)
-            join(1, 0, T)
+            for h in range(H):
+                empty_s(0, [h])
+                store(0, slice(h, h + 1))
             weigh_below(1, 3, slice(T, HALF))
+            join(1, 0, T)
+            join(2, 0, T // 2)
             quantize(1, 0, T)
             multiply(1)
-            join(2, 0, T // 2)
             join(2, T // 2, T // 2)
-            empty_s(1, [0, 1, 2, 3])
-            store(1)
+            empty_s(1, [0, 1])
+            store(1, lo)
+            empty_s(1, [2, 3])
+            store(1, hi)
             quantize(2, 0, T // 2)
             quantize(2, T // 2, T // 2)
             multiply(2)

@@ -142,9 +142,10 @@ def tile_rows_read_elu1_kernel(tc, q, qa, S, out):
             nc.scalar.dma_start(out=weight[:], in_=w_src.partition_broadcast(H))
             for js in planes:
                 load(0, js)
+            load(1, planes[0])
             nc.sync.dma_start(out=s_raw[:], in_=s_src)
-            load(1, lo)
-            load(1, hi)
+            load(1, slice(1, 3))
+            load(1, planes[3])
             for js in planes[:-1]:
                 exp(0, js)
             exp(0, planes[-1], slice(0, T))
@@ -155,27 +156,27 @@ def tile_rows_read_elu1_kernel(tc, q, qa, S, out):
                 weigh_below(0, j - 1)
             weigh_below(0, PACK - 1, slice(0, T))
             weigh_below(0, PACK - 1, slice(T, HALF))
+            exp(1, planes[0])
+            weigh_above(1, 0)
             s_interleave()
-            exp(1, lo)
-            exp(1, hi, slice(0, T))
-            exp(1, hi, slice(T, HALF))
+            exp(1, slice(1, 3))
+            exp(1, planes[3])
             join(0, 0, T)
             join(0, T, T)
             s_quantize()
             quantize(0, 0, 2 * T)
             multiply(0)
-            weigh_above(1, 0)
-            weigh_above(1, 1)
             weigh_below(1, 0)
-            weigh_below(1, 1)
+            weigh_above(1, 1)
             weigh_above(1, 2)
+            weigh_below(1, 1)
             weigh_above(1, 3)
             weigh_below(1, 2, slice(0, T))
             weigh_below(1, 3, slice(0, T))
             weigh_below(1, 2, slice(T, HALF))
-            for h in range(H):
-                empty_s(0, [h])
-                store(0, slice(h, h + 1))
+            for hs in ([0], [1], [2, 3]):
+                empty_s(0, hs)
+                store(0, slice(hs[0], hs[-1] + 1))
             weigh_below(1, 3, slice(T, HALF))
             join(1, 0, T)
             join(2, 0, T // 2)

@@ -58,8 +58,9 @@ def tile_rows_read_elu1_kernel(tc, q, qa, S, out):
             [banks[h][0][:, 2 * E : 3 * E] for h in range(H)],
         ]
 
-        def load(u, js):
-            nc.sync.dma_start(out=raw[u][:, js, :], in_=q_src[:, js, u * HALF : (u + 1) * HALF])
+        def load(u, js, c0=0, cw=HALF):
+            n0 = u * HALF + c0
+            nc.sync.dma_start(out=raw[u][:, js, c0 : c0 + cw], in_=q_src[:, js, n0 : n0 + cw])
 
         def exp(u, js, ns=slice(0, HALF)):
             nc.scalar.activation(out=expo[u][:, js, ns], in_=raw[u][:, js, ns], func=ACT.Exp)
@@ -140,8 +141,10 @@ def tile_rows_read_elu1_kernel(tc, q, qa, S, out):
         planes = [slice(j, j + 1) for j in range(PACK)]
         with tc.manual_schedule():
             nc.scalar.dma_start(out=weight[:], in_=w_src.partition_broadcast(H))
-            for js in planes:
+            for js in planes[:-1]:
                 load(0, js)
+            load(0, planes[-1], 0, T)
+            load(0, planes[-1], T, T)
             load(1, planes[0])
             nc.sync.dma_start(out=s_raw[:], in_=s_src)
             load(1, slice(1, 3))
@@ -163,10 +166,10 @@ def tile_rows_read_elu1_kernel(tc, q, qa, S, out):
             exp(1, planes[3])
             join(0, 0, T)
             join(0, T, T)
+            weigh_below(1, 0)
             s_quantize()
             quantize(0, 0, 2 * T)
             multiply(0)
-            weigh_below(1, 0)
             weigh_above(1, 1)
             weigh_above(1, 2)
             weigh_below(1, 1)
@@ -174,7 +177,7 @@ def tile_rows_read_elu1_kernel(tc, q, qa, S, out):
             weigh_below(1, 2, slice(0, T))
             weigh_below(1, 3, slice(0, T))
             weigh_below(1, 2, slice(T, HALF))
-            for hs in ([0], [1], [2, 3]):
+            for hs in ([0, 1], [2, 3]):
                 empty_s(0, hs)
                 store(0, slice(hs[0], hs[-1] + 1))
             weigh_below(1, 3, slice(T, HALF))
@@ -185,11 +188,12 @@ def tile_rows_read_elu1_kernel(tc, q, qa, S, out):
             join(2, T // 2, T // 2)
             empty_s(1, [0, 1])
             store(1, lo)
-            empty_s(1, [2, 3])
-            store(1, hi)
+            empty_s(1, [2])
             quantize(2, 0, T // 2)
             quantize(2, T // 2, T // 2)
             multiply(2)
+            empty_v(1, [3])
+            store(1, hi)
             empty_s(2, [0])
             empty_v(2, [1])
             store(2, lo)

@@ -16,54 +16,61 @@ ACT = mybir.ActivationFunctionType
 P = 128
 PACK = 4
 ROWS = D // PACK
-T = 128
-RUN = 2
+CHUNK = 128
 HALF = N // 2
+PAIR = 2
+BANK = 512
 
 
 def tile_rows_read_elu1_kernel(tc, q, qa, S, out):
     nc = tc.nc
     q_src = q.rearrange("h (p j) n -> (h p) j n", j=PACK)
     s_src = S.rearrange("h (p j) e -> (h p) j e", j=PACK)
-    w_src = qa.rearrange("(p j) o -> p (j o)", j=PACK)
-    spans = [(0, 2 * T), (2 * T, T), (3 * T, T)]
+    qa_src = qa.rearrange("(p j) o -> p (j o)", j=PACK)
+    out_by_token = out.rearrange("h n e -> n h e")
 
     with ExitStack() as ctx:
         sb = ctx.enter_context(tc.tile_pool(name="sb", bufs=1))
         ps = ctx.enter_context(tc.psum_pool(name="ps", bufs=1))
 
-        def halves(name):
+        def half_tiles(name):
             return [sb.tile([P, PACK, HALF], F32, name=name + str(u), align_bytes=64) for u in range(2)]
 
-        def tiles(name, shape, dtype):
-            return [sb.tile(shape(w), dtype, name=name + str(g), align_bytes=64) for g, (n0, w) in enumerate(spans)]
+        def token_tiles(name, inner, dtype):
+            first = sb.tile([P, HALF] + inner, dtype, name=name + "01", align_bytes=64)
+            third = sb.tile([P, CHUNK] + inner, dtype, name=name + "2", align_bytes=64)
+            fourth = sb.tile([P, CHUNK] + inner, dtype, name=name + "3", align_bytes=64)
+            return [first[:, 0:CHUNK], first[:, CHUNK:HALF], third[:], fourth[:], first[:]]
 
-        raw = halves("raw")
-        expo = halves("expo")
-        above = halves("above")
-        below = halves("below")
-        grouped = tiles("grouped", lambda w: [P, w, PACK], BF16)
-        codes = tiles("codes", lambda w: [P, w], U32)
-        scales = tiles("scales", lambda w: [P, w], U8)
-        res = tiles("res", lambda w: [P, H, (w // T) * E], F32)
+        raw = half_tiles("raw")
+        expo = half_tiles("expo")
+        above = half_tiles("above")
+        below = half_tiles("below")
+        grouped = token_tiles("grouped", [PACK], BF16)
+        codes = token_tiles("codes", [], U32)
+        scales = token_tiles("scales", [], U8)
+        first_half = N // CHUNK
+        res = [sb.tile([P, H, E], F32, name="res" + str(c), align_bytes=64) for c in range(N // CHUNK)]
         weight = sb.tile([P, PACK], F32, name="weight", align_bytes=64)
         s_raw = sb.tile([P, PACK, E], F32, name="s_raw", align_bytes=64)
         s_grouped = sb.tile([P, E, PACK], BF16, name="s_grouped", align_bytes=64)
         s_codes = sb.tile([P, E], U32, name="s_codes", align_bytes=64)
         s_scales = sb.tile([P, E], U8, name="s_scales", align_bytes=64)
-        banks = [[ps.tile([P, 512], F32, name="bank%d_%d" % (h, b)) for b in range(2)] for h in range(H)]
-        acc = [
-            [banks[h][0][:, 0 : 2 * E] for h in range(H)],
-            [banks[h][1][:, 0:E] for h in range(H)],
-            [banks[h][0][:, 2 * E : 3 * E] for h in range(H)],
-        ]
+        banks = [[ps.tile([P, BANK], F32, name="bank%d_%d" % (h, b)) for b in range(2)] for h in range(H)]
 
-        def load(u, js, c0=0, cw=HALF):
-            n0 = u * HALF + c0
-            nc.sync.dma_start(out=raw[u][:, js, c0 : c0 + cw], in_=q_src[:, js, n0 : n0 + cw])
+        def acc(c, h):
+            return banks[h][c % 2][:, (c // 2) * E : (c // 2 + 1) * E]
 
-        def exp(u, js, ns=slice(0, HALF)):
-            nc.scalar.activation(out=expo[u][:, js, ns], in_=raw[u][:, js, ns], func=ACT.Exp)
+        whole = slice(0, HALF)
+        early = slice(0, CHUNK)
+        late = slice(CHUNK, HALF)
+
+        def load(u, j0, j1, tokens=whole):
+            n0 = u * HALF
+            nc.sync.dma_start(out=raw[u][:, j0:j1, tokens], in_=q_src[:, j0:j1, n0 + tokens.start : n0 + tokens.stop])
+
+        def exp(u, j0, j1, tokens=whole):
+            nc.scalar.activation(out=expo[u][:, j0:j1, tokens], in_=raw[u][:, j0:j1, tokens], func=ACT.Exp)
 
         def weigh_above(u, j):
             nc.vector.tensor_scalar(
@@ -71,132 +78,120 @@ def tile_rows_read_elu1_kernel(tc, q, qa, S, out):
                 op0=ALU.max, op1=ALU.mult,
             )
 
-        def weigh_below(u, j, ns=slice(0, HALF)):
+        def weigh_below(u, j, tokens=whole):
             nc.vector.tensor_scalar(
-                out=below[u][:, j, ns], in0=expo[u][:, j, ns], scalar1=1.0, scalar2=weight[:, j : j + 1],
+                out=below[u][:, j, tokens], in0=expo[u][:, j, tokens], scalar1=1.0, scalar2=weight[:, j : j + 1],
                 op0=ALU.min, op1=ALU.mult,
             )
 
-        def join(g, c0, cw):
-            n0, w = spans[g]
-            u, m0 = divmod(n0 + c0, HALF)
-            if g == 0:
-                dst = grouped[g][:].rearrange("p (r s) j -> p s j r", r=RUN)[:, c0 // RUN : (c0 + cw) // RUN]
-            else:
-                dst = grouped[g][:, c0 : c0 + cw, :].rearrange("p (s r) j -> p s j r", r=RUN)
+        def join(c, t0=0, t1=CHUNK):
+            u, m0 = divmod(c * CHUNK, HALF)
             nc.vector.tensor_tensor(
-                out=dst,
-                in0=above[u][:, :, m0 : m0 + cw].rearrange("p j (s r) -> p s j r", r=RUN),
-                in1=below[u][:, :, m0 : m0 + cw].rearrange("p j (s r) -> p s j r", r=RUN),
+                out=grouped[c][:, t0:t1, :].rearrange("p (s r) j -> p s j r", r=PAIR),
+                in0=above[u][:, :, m0 + t0 : m0 + t1].rearrange("p j (s r) -> p s j r", r=PAIR),
+                in1=below[u][:, :, m0 + t0 : m0 + t1].rearrange("p j (s r) -> p s j r", r=PAIR),
                 op=ALU.add,
             )
 
-        def quantize(g, c0, cw):
+        def quantize(view, t0, t1):
             nc.vector.quantize_mx(
-                out=codes[g][:, c0 : c0 + cw].bitcast(FP8X4),
-                scales=scales[g][:, c0 : c0 + cw],
-                in_=grouped[g][:, c0 : c0 + cw, :].rearrange("p n j -> p (n j)"),
+                out=codes[view][:, t0:t1].bitcast(FP8X4),
+                scales=scales[view][:, t0:t1],
+                in_=grouped[view][:, t0:t1, :].rearrange("p n j -> p (n j)"),
             )
 
-        def multiply(g):
+        def multiply(c):
             for h in range(H):
                 rows = slice(ROWS * h, ROWS * (h + 1))
-                for r in range(spans[g][1] // T):
-                    cols = slice(r * T, (r + 1) * T)
-                    nc.tensor.matmul_mx(
-                        out=acc[g][h][:, r * E : (r + 1) * E],
-                        lhsT=codes[g][rows, cols].bitcast(FP8X4),
-                        lhsT_scale=scales[g][rows, cols],
-                        rhs=s_codes[rows, :].bitcast(FP8X4),
-                        rhs_scale=s_scales[rows, :],
-                        start=True,
-                        stop=True,
-                    )
+                nc.tensor.matmul_mx(
+                    out=acc(c, h),
+                    lhsT=codes[c][rows, :].bitcast(FP8X4),
+                    lhsT_scale=scales[c][rows, :],
+                    rhs=s_codes[rows, :].bitcast(FP8X4),
+                    rhs_scale=s_scales[rows, :],
+                    start=True,
+                    stop=True,
+                )
 
-        def empty_s(g, heads):
-            for h in heads:
-                nc.scalar.copy(out=res[g][:, h, :], in_=acc[g][h])
+        def empty_on_scalar(c, h):
+            nc.scalar.copy(out=res[c][:, h, :], in_=acc(c, h))
 
-        def empty_v(g, heads):
-            for h in heads:
-                nc.vector.tensor_copy(out=res[g][:, h, :], in_=acc[g][h])
+        def empty_on_vector(c, h):
+            nc.vector.tensor_copy(out=res[c][:, h, :], in_=acc(c, h))
 
-        def store(g, hs=slice(0, H), engine=nc.sync):
-            n0, w = spans[g]
-            dst = out[:, n0 : n0 + w, :].rearrange("h (s r) e -> s h (r e)", r=w // T)
-            engine.dma_start(out=dst[:, hs, :], in_=res[g][:, hs, :])
+        def store(c, h0, h1):
+            nc.sync.dma_start(out=out_by_token[c * CHUNK : (c + 1) * CHUNK, h0:h1, :], in_=res[c][:, h0:h1, :])
 
-        def s_interleave():
-            nc.scalar.copy(
-                out=s_grouped[:].rearrange("p (g i) j -> p g j i", i=RUN),
-                in_=s_raw[:].rearrange("p j (g i) -> p g j i", i=RUN),
-            )
-
-        def s_quantize():
-            nc.vector.quantize_mx(
-                out=s_codes[:].bitcast(FP8X4), scales=s_scales[:], in_=s_grouped[:].rearrange("p e j -> p (e j)")
-            )
-
-        lo, hi = slice(0, 2), slice(2, 4)
-        planes = [slice(j, j + 1) for j in range(PACK)]
+        last = PACK - 1
         with tc.manual_schedule():
-            nc.scalar.dma_start(out=weight[:], in_=w_src.partition_broadcast(H))
-            for js in planes[:-1]:
-                load(0, js)
-            load(0, planes[-1], 0, T)
-            load(0, planes[-1], T, T)
-            load(1, planes[0])
+            nc.scalar.dma_start(out=weight[:], in_=qa_src.partition_broadcast(H))
+            for j in range(last):
+                load(0, j, j + 1)
+            load(0, last, PACK, early)
+            load(0, last, PACK, late)
+            load(1, 0, 1)
             nc.sync.dma_start(out=s_raw[:], in_=s_src)
-            load(1, slice(1, 3))
-            load(1, planes[3])
-            for js in planes[:-1]:
-                exp(0, js)
-            exp(0, planes[-1], slice(0, T))
-            exp(0, planes[-1], slice(T, HALF))
+            load(1, 1, last)
+            load(1, last, PACK)
+
+            for j in range(last):
+                exp(0, j, j + 1)
+            exp(0, last, PACK, early)
+            exp(0, last, PACK, late)
+            exp(1, 0, 1)
+            nc.scalar.copy(
+                out=s_grouped[:].rearrange("p (g i) j -> p g j i", i=PAIR),
+                in_=s_raw[:].rearrange("p j (g i) -> p g j i", i=PAIR),
+            )
+            exp(1, 1, last)
+            exp(1, last, PACK)
+
             weigh_above(0, 0)
             for j in range(1, PACK):
                 weigh_above(0, j)
-                weigh_below(0, j - 1)
-            weigh_below(0, PACK - 1, slice(0, T))
-            weigh_below(0, PACK - 1, slice(T, HALF))
-            exp(1, planes[0])
+                if j < last:
+                    weigh_below(0, j - 1)
+            weigh_below(0, last - 1)
+            weigh_below(0, last, early)
+            weigh_below(0, last, late)
             weigh_above(1, 0)
-            s_interleave()
-            exp(1, slice(1, 3))
-            exp(1, planes[3])
-            join(0, 0, T)
-            join(0, T, T)
+            join(0)
+            join(1)
             weigh_below(1, 0)
-            s_quantize()
-            quantize(0, 0, 2 * T)
-            multiply(0)
+            nc.vector.quantize_mx(
+                out=s_codes[:].bitcast(FP8X4), scales=s_scales[:], in_=s_grouped[:].rearrange("p e j -> p (e j)")
+            )
+            quantize(first_half, 0, HALF)
+            for c in (0, 1):
+                multiply(c)
+            for c in (0, 1):
+                for h in range(H):
+                    empty_on_scalar(c, h)
+                store(c, 0, H)
+
             weigh_above(1, 1)
             weigh_above(1, 2)
             weigh_below(1, 1)
-            weigh_above(1, 3)
-            weigh_below(1, 2, slice(0, T))
-            weigh_below(1, 3, slice(0, T))
-            weigh_below(1, 2, slice(T, HALF))
-            for hs in ([0, 1], [2, 3]):
-                empty_s(0, hs)
-                store(0, slice(hs[0], hs[-1] + 1))
-            weigh_below(1, 3, slice(T, HALF))
-            join(1, 0, T)
-            join(2, 0, T // 2)
-            quantize(1, 0, T)
-            multiply(1)
-            join(2, T // 2, T // 2)
-            empty_s(1, [0, 1])
-            store(1, lo)
-            empty_s(1, [2])
-            quantize(2, 0, T // 2)
-            quantize(2, T // 2, T // 2)
+            weigh_above(1, last)
+            for tokens in (early, late):
+                weigh_below(1, 2, tokens)
+                weigh_below(1, last, tokens)
+            join(2)
+            join(3, 0, CHUNK // 2)
+            quantize(2, 0, CHUNK)
             multiply(2)
-            empty_v(1, [3])
-            store(1, hi)
-            empty_s(2, [0])
-            empty_v(2, [1])
-            store(2, lo)
-            empty_s(2, [2])
-            empty_v(2, [3])
-            store(2, hi)
+            join(3, CHUNK // 2, CHUNK)
+            quantize(3, 0, CHUNK // 2)
+            quantize(3, CHUNK // 2, CHUNK)
+            multiply(3)
+
+            for h in range(H - 1):
+                empty_on_scalar(2, h)
+                if h == 1:
+                    store(2, 0, 2)
+            empty_on_vector(2, H - 1)
+            store(2, 2, H)
+            for h in (0, 2):
+                empty_on_scalar(3, h)
+                empty_on_vector(3, h + 1)
+                store(3, h, h + 2)

@@ -144,7 +144,8 @@ def tile_rows_read_elu1_kernel(tc, q, qa, S, out):
                 in_=s_raw[:].rearrange("p j (g i) -> p g j i", i=PAIR),
             )
             exp(1, 1, last)
-            exp(1, last, PACK)
+            exp(1, last, PACK, early)
+            exp(1, last, PACK, late)
 
             weigh_above(0, 0)
             for j in range(1, PACK):
@@ -153,29 +154,32 @@ def tile_rows_read_elu1_kernel(tc, q, qa, S, out):
                     weigh_below(0, j - 1)
             weigh_below(0, last - 1)
             weigh_below(0, last, early)
-            weigh_below(0, last, late)
             weigh_above(1, 0)
+            weigh_below(0, last, late)
             join(0)
             join(1)
             weigh_below(1, 0)
             nc.vector.quantize_mx(
                 out=s_codes[:].bitcast(FP8X4), scales=s_scales[:], in_=s_grouped[:].rearrange("p e j -> p (e j)")
             )
-            quantize(first_half, 0, HALF)
-            for c in (0, 1):
-                multiply(c)
-            for c in (0, 1):
-                for h in range(H):
-                    empty_on_scalar(c, h)
-                store(c, 0, H)
+            quantize(0, 0, CHUNK)
+            multiply(0)
+            for h in range(H):
+                empty_on_scalar(0, h)
+            store(0, 0, H)
 
             weigh_above(1, 1)
             weigh_above(1, 2)
             weigh_below(1, 1)
             weigh_above(1, last)
-            for tokens in (early, late):
-                weigh_below(1, 2, tokens)
-                weigh_below(1, last, tokens)
+            weigh_below(1, 2)
+            weigh_below(1, last, early)
+            weigh_below(1, last, late)
+            quantize(1, 0, CHUNK)
+            multiply(1)
+            for h in range(H):
+                empty_on_scalar(1, h)
+            store(1, 0, H)
             join(2)
             join(3, 0, CHUNK // 2)
             quantize(2, 0, CHUNK)

@@ -52,6 +52,7 @@ def tile_rows_read_elu1_kernel(tc, q, qa, S, out):
         first_half = N // CHUNK
         res = [sb.tile([P, H, E], F32, name="res" + str(c), align_bytes=64) for c in range(N // CHUNK)]
         weight = sb.tile([P, PACK], F32, name="weight", align_bytes=64)
+        positive = sb.tile([P, PACK, CHUNK], F32, name="positive", align_bytes=64)
         s_raw = sb.tile([P, PACK, E], F32, name="s_raw", align_bytes=64)
         s_grouped = sb.tile([P, E, PACK], BF16, name="s_grouped", align_bytes=64)
         s_codes = sb.tile([P, E], U32, name="s_codes", align_bytes=64)
@@ -72,9 +73,18 @@ def tile_rows_read_elu1_kernel(tc, q, qa, S, out):
         def exp(u, j0, j1, tokens=whole):
             nc.scalar.activation(out=expo[u][:, j0:j1, tokens], in_=raw[u][:, j0:j1, tokens], func=ACT.Exp)
 
-        def weigh_above(u, j):
+        def rectify_on_scalar(u, j0, j1, tokens):
+            nc.scalar.activation(out=positive[:, j0:j1, :], in_=raw[u][:, j0:j1, tokens], func=ACT.Relu)
+
+        def weigh_above_on_scalar(u, j0, j1, tokens):
+            for j in range(j0, j1):
+                nc.scalar.activation(
+                    out=above[u][:, j, tokens], in_=positive[:, j, :], func=ACT.Copy, scale=weight[:, j : j + 1]
+                )
+
+        def weigh_above(u, j, tokens=whole):
             nc.vector.tensor_scalar(
-                out=above[u][:, j, :], in0=raw[u][:, j, :], scalar1=0.0, scalar2=weight[:, j : j + 1],
+                out=above[u][:, j, tokens], in0=raw[u][:, j, tokens], scalar1=0.0, scalar2=weight[:, j : j + 1],
                 op0=ALU.max, op1=ALU.mult,
             )
 
@@ -125,10 +135,8 @@ def tile_rows_read_elu1_kernel(tc, q, qa, S, out):
         last = PACK - 1
         with tc.manual_schedule():
             nc.scalar.dma_start(out=weight[:], in_=qa_src.partition_broadcast(H))
-            for j in range(last):
+            for j in range(PACK):
                 load(0, j, j + 1)
-            load(0, last, PACK, early)
-            load(0, last, PACK, late)
             load(1, 0, 1)
             nc.sync.dma_start(out=s_raw[:], in_=s_src)
             load(1, 1, last)
@@ -146,6 +154,9 @@ def tile_rows_read_elu1_kernel(tc, q, qa, S, out):
             exp(1, 1, last)
             exp(1, last, PACK, early)
             exp(1, last, PACK, late)
+            rectify_on_scalar(1, 1, last, late)
+            rectify_on_scalar(1, last, PACK, late)
+            weigh_above_on_scalar(1, 1, PACK, late)
 
             weigh_above(0, 0)
             for j in range(1, PACK):
@@ -166,12 +177,13 @@ def tile_rows_read_elu1_kernel(tc, q, qa, S, out):
             multiply(0)
             for h in range(H):
                 empty_on_scalar(0, h)
-            store(0, 0, H)
+                if h % 2 == 1:
+                    store(0, h - 1, h + 1)
 
-            weigh_above(1, 1)
-            weigh_above(1, 2)
+            weigh_above(1, 1, early)
+            weigh_above(1, 2, early)
             weigh_below(1, 1)
-            weigh_above(1, last)
+            weigh_above(1, last, early)
             weigh_below(1, 2)
             weigh_below(1, last, early)
             weigh_below(1, last, late)
@@ -189,13 +201,8 @@ def tile_rows_read_elu1_kernel(tc, q, qa, S, out):
             quantize(3, CHUNK // 2, CHUNK)
             multiply(3)
 
-            for h in range(H - 1):
-                empty_on_scalar(2, h)
-                if h == 1:
-                    store(2, 0, 2)
-            empty_on_vector(2, H - 1)
-            store(2, 2, H)
-            for h in (0, 2):
-                empty_on_scalar(3, h)
-                empty_on_vector(3, h + 1)
-                store(3, h, h + 2)
+            for c in (2, 3):
+                for h in (0, 2):
+                    empty_on_scalar(c, h)
+                    empty_on_vector(c, h + 1)
+                    store(c, h, h + 2)

@@ -52,7 +52,7 @@ def tile_rows_read_elu1_kernel(tc, q, qa, S, out):
         first_half = N // CHUNK
         res = [sb.tile([P, H, E], F32, name="res" + str(c), align_bytes=64) for c in range(N // CHUNK)]
         weight = sb.tile([P, PACK], F32, name="weight", align_bytes=64)
-        positive = sb.tile([P, PACK, CHUNK], F32, name="positive", align_bytes=64)
+        positive = sb.tile([P, PACK, CHUNK // 2], F32, name="positive", align_bytes=64)
         s_raw = sb.tile([P, PACK, E], F32, name="s_raw", align_bytes=64)
         s_grouped = sb.tile([P, E, PACK], BF16, name="s_grouped", align_bytes=64)
         s_codes = sb.tile([P, E], U32, name="s_codes", align_bytes=64)
@@ -65,6 +65,8 @@ def tile_rows_read_elu1_kernel(tc, q, qa, S, out):
         whole = slice(0, HALF)
         early = slice(0, CHUNK)
         late = slice(CHUNK, HALF)
+        front = slice(0, HALF - CHUNK // 2)
+        back = slice(HALF - CHUNK // 2, HALF)
 
         def load(u, j0, j1, tokens=whole):
             n0 = u * HALF
@@ -154,9 +156,9 @@ def tile_rows_read_elu1_kernel(tc, q, qa, S, out):
             exp(1, 1, last)
             exp(1, last, PACK, early)
             exp(1, last, PACK, late)
-            rectify_on_scalar(1, 1, last, late)
-            rectify_on_scalar(1, last, PACK, late)
-            weigh_above_on_scalar(1, 1, PACK, late)
+            rectify_on_scalar(1, 1, last, back)
+            rectify_on_scalar(1, last, PACK, back)
+            weigh_above_on_scalar(1, 1, PACK, back)
 
             weigh_above(0, 0)
             for j in range(1, PACK):
@@ -180,10 +182,10 @@ def tile_rows_read_elu1_kernel(tc, q, qa, S, out):
                 if h % 2 == 1:
                     store(0, h - 1, h + 1)
 
-            weigh_above(1, 1, early)
-            weigh_above(1, 2, early)
+            weigh_above(1, 1, front)
+            weigh_above(1, 2, front)
             weigh_below(1, 1)
-            weigh_above(1, last, early)
+            weigh_above(1, last, front)
             weigh_below(1, 2)
             weigh_below(1, last, early)
             weigh_below(1, last, late)

@@ -20,6 +20,8 @@ CHUNK = 128
 HALF = N // 2
 PAIR = 2
 BANK = 512
+BANK_OF = ((0, 0, 0, 1), (0, 0, 1, 0), (0, 1, 0, 1), (0, 1, 0, 1))
+HEAD_ORDER = ((0, 1, 2, 3), (2, 0, 1, 3), (1, 0, 2, 3), (0, 1, 2, 3))
 
 
 def tile_rows_read_elu1_kernel(tc, q, qa, S, out):
@@ -60,7 +62,7 @@ def tile_rows_read_elu1_kernel(tc, q, qa, S, out):
         banks = [[ps.tile([P, BANK], F32, name="bank%d_%d" % (h, b)) for b in range(2)] for h in range(H)]
 
         def acc(c, h):
-            return banks[h][c % 2][:, (c // 2) * E : (c // 2 + 1) * E]
+            return banks[h][BANK_OF[h][c]][:, c * E : (c + 1) * E]
 
         whole = slice(0, HALF)
         early = slice(0, CHUNK)
@@ -113,7 +115,7 @@ def tile_rows_read_elu1_kernel(tc, q, qa, S, out):
             )
 
         def multiply(c):
-            for h in range(H):
+            for h in HEAD_ORDER[c]:
                 rows = slice(ROWS * h, ROWS * (h + 1))
                 nc.tensor.matmul_mx(
                     out=acc(c, h),
@@ -191,7 +193,7 @@ def tile_rows_read_elu1_kernel(tc, q, qa, S, out):
             weigh_below(1, last, late)
             quantize(1, 0, CHUNK)
             multiply(1)
-            for h in range(H):
+            for h in HEAD_ORDER[1]:
                 empty_on_scalar(1, h)
             store(1, 0, H)
             join(2)
@@ -205,6 +207,6 @@ def tile_rows_read_elu1_kernel(tc, q, qa, S, out):
 
             for c in (2, 3):
                 for h in (0, 2):
-                    empty_on_scalar(c, h)
-                    empty_on_vector(c, h + 1)
+                    empty_on_scalar(c, HEAD_ORDER[c][h])
+                    empty_on_vector(c, HEAD_ORDER[c][h + 1])
                     store(c, h, h + 2)

@@ -74,6 +74,9 @@ def tile_rows_read_elu1_kernel(tc, q, qa, S, out):
             n0 = u * HALF
             nc.sync.dma_start(out=raw[u][:, j0:j1, tokens], in_=q_src[:, j0:j1, n0 + tokens.start : n0 + tokens.stop])
 
+        def load_weight(queue, h):
+            queue.dma_start(out=weight[ROWS * h : ROWS * (h + 1), :], in_=qa_src)
+
         def exp(u, j0, j1, tokens=whole):
             nc.scalar.activation(out=expo[u][:, j0:j1, tokens], in_=raw[u][:, j0:j1, tokens], func=ACT.Exp)
 
@@ -138,24 +141,27 @@ def tile_rows_read_elu1_kernel(tc, q, qa, S, out):
 
         last = PACK - 1
         with tc.manual_schedule():
-            nc.scalar.dma_start(out=weight[:], in_=qa_src.partition_broadcast(H))
-            for j in range(PACK):
-                load(0, j, j + 1)
-            load(1, 0, 1)
+            load_weight(nc.scalar, 0)
+            load_weight(nc.scalar, 1)
+            load(0, 0, 2)
+            load_weight(nc.sync, 2)
+            load_weight(nc.sync, 3)
+            load(0, 2, last)
+            load(0, last, PACK)
+            load(1, 0, 2)
             nc.sync.dma_start(out=s_raw[:], in_=s_src)
-            load(1, 1, last)
-            load(1, last, PACK)
+            load(1, 2, PACK)
 
             for j in range(last):
                 exp(0, j, j + 1)
             exp(0, last, PACK, early)
             exp(0, last, PACK, late)
-            exp(1, 0, 1)
+            exp(1, 0, 2)
             nc.scalar.copy(
                 out=s_grouped[:].rearrange("p (g i) j -> p g j i", i=PAIR),
                 in_=s_raw[:].rearrange("p j (g i) -> p g j i", i=PAIR),
             )
-            exp(1, 1, last)
+            exp(1, 2, last)
             exp(1, last, PACK, early)
             exp(1, last, PACK, late)
             rectify_on_scalar(1, 1, last, back)
@@ -163,14 +169,14 @@ def tile_rows_read_elu1_kernel(tc, q, qa, S, out):
             weigh_above_on_scalar(1, 1, PACK, back)
 
             weigh_above(0, 0)
-            for j in range(1, PACK):
+            weigh_above(0, 1)
+            for j in range(2, PACK):
                 weigh_above(0, j)
-                if j < last:
-                    weigh_below(0, j - 1)
+                weigh_below(0, j - 2)
             weigh_below(0, last - 1)
             weigh_below(0, last, early)
-            weigh_above(1, 0)
             weigh_below(0, last, late)
+            weigh_above(1, 0)
             join(0)
             join(1)
             weigh_below(1, 0)
@@ -181,8 +187,7 @@ def tile_rows_read_elu1_kernel(tc, q, qa, S, out):
             multiply(0)
             for h in range(H):
                 empty_on_scalar(0, h)
-                if h % 2 == 1:
-                    store(0, h - 1, h + 1)
+            store(0, 0, H)
 
             weigh_above(1, 1, front)
             weigh_above(1, 2, front)
@@ -205,8 +210,11 @@ def tile_rows_read_elu1_kernel(tc, q, qa, S, out):
             quantize(3, CHUNK // 2, CHUNK)
             multiply(3)
 
-            for c in (2, 3):
-                for h in (0, 2):
-                    empty_on_scalar(c, HEAD_ORDER[c][h])
-                    empty_on_vector(c, HEAD_ORDER[c][h + 1])
-                    store(c, h, h + 2)
+            for h in (0, 2):
+                empty_on_scalar(2, HEAD_ORDER[2][h])
+                empty_on_vector(2, HEAD_ORDER[2][h + 1])
+                store(2, h, h + 2)
+            for h in (0, 2):
+                empty_on_vector(3, h)
+                empty_on_scalar(3, h + 1)
+                store(3, h, h + 2)

@@ -150,7 +150,8 @@ def tile_rows_read_elu1_kernel(tc, q, qa, S, out):
             load(0, last, PACK)
             load(1, 0, 2)
             nc.sync.dma_start(out=s_raw[:], in_=s_src)
-            load(1, 2, PACK)
+            load(1, 2, last)
+            load(1, last, PACK)
 
             for j in range(last):
                 exp(0, j, j + 1)
@@ -187,7 +188,7 @@ def tile_rows_read_elu1_kernel(tc, q, qa, S, out):
             multiply(0)
             for h in range(H):
                 empty_on_scalar(0, h)
-            store(0, 0, H)
+                store(0, h, h + 1)
 
             weigh_above(1, 1, front)
             weigh_above(1, 2, front)
@@ -200,7 +201,7 @@ def tile_rows_read_elu1_kernel(tc, q, qa, S, out):
             multiply(1)
             for h in HEAD_ORDER[1]:
                 empty_on_scalar(1, h)
-            store(1, 0, H)
+                store(1, h, h + 1)
             join(2)
             join(3, 0, CHUNK // 2)
             quantize(2, 0, CHUNK)
@@ -210,10 +211,13 @@ def tile_rows_read_elu1_kernel(tc, q, qa, S, out):
             quantize(3, CHUNK // 2, CHUNK)
             multiply(3)
 
-            for h in (0, 2):
-                empty_on_scalar(2, HEAD_ORDER[2][h])
-                empty_on_vector(2, HEAD_ORDER[2][h + 1])
-                store(2, h, h + 2)
+            empty_on_scalar(2, 1)
+            store(2, 1, 2)
+            empty_on_vector(2, 0)
+            store(2, 0, 1)
+            empty_on_scalar(2, 2)
+            empty_on_vector(2, 3)
+            store(2, 2, 4)
             for h in (0, 2):
                 empty_on_vector(3, h)
                 empty_on_scalar(3, h + 1)

@@ -181,18 +181,18 @@ def tile_rows_read_elu1_kernel(tc, q, qa, S, out):
             join(0)
             join(1)
             weigh_below(1, 0)
+            quantize(0, 0, CHUNK)
+            weigh_above(1, 1, front)
+            weigh_below(1, 1)
             nc.vector.quantize_mx(
                 out=s_codes[:].bitcast(FP8X4), scales=s_scales[:], in_=s_grouped[:].rearrange("p e j -> p (e j)")
             )
-            quantize(0, 0, CHUNK)
             multiply(0)
             for h in range(H):
                 empty_on_scalar(0, h)
                 store(0, h, h + 1)
 
-            weigh_above(1, 1, front)
             weigh_above(1, 2, front)
-            weigh_below(1, 1)
             weigh_above(1, last, front)
             weigh_below(1, 2)
             weigh_below(1, last, early)

@@ -54,7 +54,7 @@ def tile_rows_read_elu1_kernel(tc, q, qa, S, out):
         first_half = N // CHUNK
         res = [sb.tile([P, H, E], F32, name="res" + str(c), align_bytes=64) for c in range(N // CHUNK)]
         weight = sb.tile([P, PACK], F32, name="weight", align_bytes=64)
-        positive = sb.tile([P, PACK, CHUNK // 2], F32, name="positive", align_bytes=64)
+        positive = sb.tile([P, PACK, CHUNK], F32, name="positive", align_bytes=64)
         s_raw = sb.tile([P, PACK, E], F32, name="s_raw", align_bytes=64)
         s_grouped = sb.tile([P, E, PACK], BF16, name="s_grouped", align_bytes=64)
         s_codes = sb.tile([P, E], U32, name="s_codes", align_bytes=64)
@@ -81,12 +81,12 @@ def tile_rows_read_elu1_kernel(tc, q, qa, S, out):
             nc.scalar.activation(out=expo[u][:, j0:j1, tokens], in_=raw[u][:, j0:j1, tokens], func=ACT.Exp)
 
         def rectify_on_scalar(u, j0, j1, tokens):
-            nc.scalar.activation(out=positive[:, j0:j1, :], in_=raw[u][:, j0:j1, tokens], func=ACT.Relu)
+            nc.scalar.activation(out=positive[:, j0:j1, 0 : tokens.stop - tokens.start], in_=raw[u][:, j0:j1, tokens], func=ACT.Relu)
 
         def weigh_above_on_scalar(u, j0, j1, tokens):
             for j in range(j0, j1):
                 nc.scalar.activation(
-                    out=above[u][:, j, tokens], in_=positive[:, j, :], func=ACT.Copy, scale=weight[:, j : j + 1]
+                    out=above[u][:, j, tokens], in_=positive[:, j, 0 : tokens.stop - tokens.start], func=ACT.Copy, scale=weight[:, j : j + 1]
                 )
 
         def weigh_above(u, j, tokens=whole):
@@ -157,7 +157,9 @@ def tile_rows_read_elu1_kernel(tc, q, qa, S, out):
                 exp(0, j, j + 1)
             exp(0, last, PACK, early)
             exp(0, last, PACK, late)
+            rectify_on_scalar(1, 1, 2, late)
             exp(1, 0, 2)
+            weigh_above_on_scalar(1, 1, 2, late)
             nc.scalar.copy(
                 out=s_grouped[:].rearrange("p (g i) j -> p g j i", i=PAIR),
                 in_=s_raw[:].rearrange("p j (g i) -> p g j i", i=PAIR),
@@ -165,9 +167,9 @@ def tile_rows_read_elu1_kernel(tc, q, qa, S, out):
             exp(1, 2, last)
             exp(1, last, PACK, early)
             exp(1, last, PACK, late)
-            rectify_on_scalar(1, 1, last, back)
+            rectify_on_scalar(1, 2, last, back)
             rectify_on_scalar(1, last, PACK, back)
-            weigh_above_on_scalar(1, 1, PACK, back)
+            weigh_above_on_scalar(1, 2, PACK, back)
 
             weigh_above(0, 0)
             weigh_above(0, 1)
@@ -182,8 +184,7 @@ def tile_rows_read_elu1_kernel(tc, q, qa, S, out):
             join(1)
             weigh_below(1, 0)
             quantize(0, 0, CHUNK)
-            weigh_above(1, 1, front)
-            weigh_below(1, 1)
+            weigh_above(1, 1, early)
             nc.vector.quantize_mx(
                 out=s_codes[:].bitcast(FP8X4), scales=s_scales[:], in_=s_grouped[:].rearrange("p e j -> p (e j)")
             )
@@ -192,6 +193,7 @@ def tile_rows_read_elu1_kernel(tc, q, qa, S, out):
                 empty_on_scalar(0, h)
                 store(0, h, h + 1)
 
+            weigh_below(1, 1)
             weigh_above(1, 2, front)
             weigh_above(1, last, front)
             weigh_below(1, 2)

from contextlib import ExitStack

import concourse.mybir as mybir

H, D, N, E = 4, 128, 512, 128
FLOPS = 2 * H * D * N * E

F32 = mybir.dt.float32
BF16 = mybir.dt.bfloat16
U32 = mybir.dt.uint32
U8 = mybir.dt.uint8
FP8X4 = mybir.dt.float8_e4m3fn_x4
ALU = mybir.AluOpType
ACT = mybir.ActivationFunctionType

P = 128
PACK = 4
ROWS = D // PACK
CHUNK = 128
HALF = N // 2
PAIR = 2
BANK = 512
BANK_OF = ((0, 0, 0, 1), (0, 0, 1, 0), (0, 1, 0, 1), (0, 1, 0, 1))
HEAD_ORDER = ((0, 1, 2, 3), (2, 0, 1, 3), (1, 0, 2, 3), (0, 1, 2, 3))


def tile_rows_read_elu1_kernel(tc, q, qa, S, out):
    nc = tc.nc
    q_src = q.rearrange("h (p j) n -> (h p) j n", j=PACK)
    s_src = S.rearrange("h (p j) e -> (h p) j e", j=PACK)
    qa_src = qa.rearrange("(p j) o -> p (j o)", j=PACK)
    out_by_token = out.rearrange("h n e -> n h e")

    with ExitStack() as ctx:
        sb = ctx.enter_context(tc.tile_pool(name="sb", bufs=1))
        ps = ctx.enter_context(tc.psum_pool(name="ps", bufs=1))

        def half_tiles(name):
            return [sb.tile([P, PACK, HALF], F32, name=name + str(u), align_bytes=64) for u in range(2)]

        def token_tiles(name, inner, dtype):
            first = sb.tile([P, HALF] + inner, dtype, name=name + "01", align_bytes=64)
            third = sb.tile([P, CHUNK] + inner, dtype, name=name + "2", align_bytes=64)
            fourth = sb.tile([P, CHUNK] + inner, dtype, name=name + "3", align_bytes=64)
            return [first[:, 0:CHUNK], first[:, CHUNK:HALF], third[:], fourth[:], first[:]]

        raw = half_tiles("raw")
        expo = half_tiles("expo")
        above = half_tiles("above")
        below = half_tiles("below")
        grouped = token_tiles("grouped", [PACK], BF16)
        codes = token_tiles("codes", [], U32)
        scales = token_tiles("scales", [], U8)
        first_half = N // CHUNK
        res = [sb.tile([P, H, E], F32, name="res" + str(c), align_bytes=64) for c in range(N // CHUNK)]
        weight = sb.tile([P, PACK], F32, name="weight", align_bytes=64)
        positive = sb.tile([P, PACK, CHUNK], F32, name="positive", align_bytes=64)
        s_raw = sb.tile([P, PACK, E], F32, name="s_raw", align_bytes=64)
        s_grouped = sb.tile([P, E, PACK], BF16, name="s_grouped", align_bytes=64)
        s_codes = sb.tile([P, E], U32, name="s_codes", align_bytes=64)
        s_scales = sb.tile([P, E], U8, name="s_scales", align_bytes=64)
        banks = [[ps.tile([P, BANK], F32, name="bank%d_%d" % (h, b)) for b in range(2)] for h in range(H)]

        def acc(c, h):
            return banks[h][BANK_OF[h][c]][:, c * E : (c + 1) * E]

        whole = slice(0, HALF)
        early = slice(0, CHUNK)
        late = slice(CHUNK, HALF)
        front = slice(0, HALF - CHUNK // 2)
        back = slice(HALF - CHUNK // 2, HALF)

        def load(u, j0, j1, tokens=whole):
            n0 = u * HALF
            nc.sync.dma_start(out=raw[u][:, j0:j1, tokens], in_=q_src[:, j0:j1, n0 + tokens.start : n0 + tokens.stop])

        def load_weight(queue, h):
            queue.dma_start(out=weight[ROWS * h : ROWS * (h + 1), :], in_=qa_src)

        def exp(u, j0, j1, tokens=whole):
            nc.scalar.activation(out=expo[u][:, j0:j1, tokens], in_=raw[u][:, j0:j1, tokens], func=ACT.Exp)

        def rectify_on_scalar(u, j0, j1, tokens):
            nc.scalar.activation(out=positive[:, j0:j1, 0 : tokens.stop - tokens.start], in_=raw[u][:, j0:j1, tokens], func=ACT.Relu)

        def weigh_above_on_scalar(u, j0, j1, tokens):
            for j in range(j0, j1):
                nc.scalar.activation(
                    out=above[u][:, j, tokens], in_=positive[:, j, 0 : tokens.stop - tokens.start], func=ACT.Copy, scale=weight[:, j : j + 1]
                )

        def weigh_above(u, j, tokens=whole):
            nc.vector.tensor_scalar(
                out=above[u][:, j, tokens], in0=raw[u][:, j, tokens], scalar1=0.0, scalar2=weight[:, j : j + 1],
                op0=ALU.max, op1=ALU.mult,
            )

        def weigh_below(u, j, tokens=whole):
            nc.vector.tensor_scalar(
                out=below[u][:, j, tokens], in0=expo[u][:, j, tokens], scalar1=1.0, scalar2=weight[:, j : j + 1],
                op0=ALU.min, op1=ALU.mult,
            )

        def join(c, t0=0, t1=CHUNK):
            u, m0 = divmod(c * CHUNK, HALF)
            nc.vector.tensor_tensor(
                out=grouped[c][:, t0:t1, :].rearrange("p (s r) j -> p s j r", r=PAIR),
                in0=above[u][:, :, m0 + t0 : m0 + t1].rearrange("p j (s r) -> p s j r", r=PAIR),
                in1=below[u][:, :, m0 + t0 : m0 + t1].rearrange("p j (s r) -> p s j r", r=PAIR),
                op=ALU.add,
            )

        def quantize(view, t0, t1):
            nc.vector.quantize_mx(
                out=codes[view][:, t0:t1].bitcast(FP8X4),
                scales=scales[view][:, t0:t1],
                in_=grouped[view][:, t0:t1, :].rearrange("p n j -> p (n j)"),
            )

        def multiply(c):
            for h in HEAD_ORDER[c]:
                rows = slice(ROWS * h, ROWS * (h + 1))
                nc.tensor.matmul_mx(
                    out=acc(c, h),
                    lhsT=codes[c][rows, :].bitcast(FP8X4),
                    lhsT_scale=scales[c][rows, :],
                    rhs=s_codes[rows, :].bitcast(FP8X4),
                    rhs_scale=s_scales[rows, :],
                    start=True,
                    stop=True,
                )

        def empty_on_scalar(c, h):
            nc.scalar.copy(out=res[c][:, h, :], in_=acc(c, h))

        def empty_on_vector(c, h):
            nc.vector.tensor_copy(out=res[c][:, h, :], in_=acc(c, h))

        def store(c, h0, h1):
            nc.sync.dma_start(out=out_by_token[c * CHUNK : (c + 1) * CHUNK, h0:h1, :], in_=res[c][:, h0:h1, :])

        last = PACK - 1
        with tc.manual_schedule():
            load_weight(nc.scalar, 0)
            load_weight(nc.scalar, 1)
            load(0, 0, 2)
            load_weight(nc.sync, 2)
            load_weight(nc.sync, 3)
            load(0, 2, last)
            load(0, last, PACK)
            load(1, 0, 2)
            nc.sync.dma_start(out=s_raw[:], in_=s_src)
            load(1, 2, last)
            load(1, last, PACK)

            for j in range(last):
                exp(0, j, j + 1)
            exp(0, last, PACK, early)
            exp(0, last, PACK, late)
            rectify_on_scalar(1, 1, 2, late)
            exp(1, 0, 2)
            weigh_above_on_scalar(1, 1, 2, late)
            nc.scalar.copy(
                out=s_grouped[:].rearrange("p (g i) j -> p g j i", i=PAIR),
                in_=s_raw[:].rearrange("p j (g i) -> p g j i", i=PAIR),
            )
            exp(1, 2, last)
            exp(1, last, PACK, early)
            exp(1, last, PACK, late)
            rectify_on_scalar(1, 2, last, back)
            rectify_on_scalar(1, last, PACK, back)
            weigh_above_on_scalar(1, 2, PACK, back)

            weigh_above(0, 0)
            weigh_above(0, 1)
            for j in range(2, PACK):
                weigh_above(0, j)
                weigh_below(0, j - 2)
            weigh_below(0, last - 1)
            weigh_below(0, last, early)
            weigh_below(0, last, late)
            weigh_above(1, 0)
            join(0)
            join(1)
            weigh_below(1, 0)
            quantize(0, 0, CHUNK)
            weigh_above(1, 1, early)
            nc.vector.quantize_mx(
                out=s_codes[:].bitcast(FP8X4), scales=s_scales[:], in_=s_grouped[:].rearrange("p e j -> p (e j)")
            )
            multiply(0)
            for h in range(H):
                empty_on_scalar(0, h)
                store(0, h, h + 1)

            weigh_below(1, 1)
            weigh_above(1, 2, front)
            weigh_above(1, last, front)
            weigh_below(1, 2)
            weigh_below(1, last, early)
            weigh_below(1, last, late)
            quantize(1, 0, CHUNK)
            multiply(1)
            for h in HEAD_ORDER[1]:
                empty_on_scalar(1, h)
                store(1, h, h + 1)
            join(2)
            join(3, 0, CHUNK // 2)
            quantize(2, 0, CHUNK)
            multiply(2)
            join(3, CHUNK // 2, CHUNK)
            quantize(3, 0, CHUNK // 2)
            quantize(3, CHUNK // 2, CHUNK)
            multiply(3)

            empty_on_scalar(2, 1)
            store(2, 1, 2)
            empty_on_vector(2, 0)
            store(2, 0, 1)
            empty_on_scalar(2, 2)
            empty_on_vector(2, 3)
            store(2, 2, 4)
            for h in (0, 2):
                empty_on_vector(3, h)
                empty_on_scalar(3, h + 1)
                store(3, h, h + 2)
